import numpy as np
import ml_dtypes


def mxq(x, axis, fmt="e4m3"):
    dtype, down = {"e4m3": (ml_dtypes.float8_e4m3fn, 7), "e5m2": (ml_dtypes.float8_e5m2, 14)}[fmt]
    v = np.moveaxis(np.asarray(x, np.float32).astype(ml_dtypes.bfloat16).astype(np.float64), axis, -1)
    blocks = v.reshape(v.shape[:-1] + (-1, 32))
    amax = np.abs(blocks).max(-1, keepdims=True)
    byte = np.maximum(np.where(amax > 0, np.frexp(amax)[1] - 1 + 127, 0) - down, 1)
    scale = np.exp2(byte - 127.0)
    codes = (blocks / scale).astype(np.float32).astype(dtype).astype(np.float64)
    return np.moveaxis((codes * scale).reshape(v.shape), -1, axis)


WIDE = False


def mx_kscale(k):
    if not WIDE:
        return np.ones(k)
    levels = np.array([10, -10, 5, -5, 0])
    if k % 512:
        return np.exp2(np.random.permutation(np.resize(levels, k // 32))).repeat(32)
    a = np.empty((k // 512, 16))
    for p in range(k // 512):
        a[p, :8] = np.random.permutation(np.resize(levels, 8))
        for g in range(8):
            far = levels[np.abs(levels - a[p, g]) >= 10]
            a[p, g + 8] = far[np.random.randint(len(far))]
    return np.exp2(a.ravel()).repeat(32)


def f64(x):
    return np.asarray(x).astype(np.float64)


def striped(idx):
    return np.tile(idx.reshape(-1, 16).T, (8, 1)).astype(np.uint16)


def unstriped(offs):
    return offs[:16].T.reshape(-1).astype(np.int64)


E2M1 = np.array([0.0, 0.5, 1.0, 1.5, 2.0, 3.0, 4.0, 6.0, -0.0, -0.5, -1.0, -1.5, -2.0, -3.0, -4.0, -6.0])


def pack_weight(w, fmt):
    k, n = w.shape
    w = f64(np.asarray(w, np.float32).astype(ml_dtypes.bfloat16)).reshape(k // 32, 32, n)
    amax = np.abs(w).max(1)
    if fmt == "e4m3":
        byte = np.frexp(amax)[1] - 1 + 127 - 7
    else:
        mant, ex = np.frexp(amax / 6.0)
        byte = np.where(mant > 0.5, ex, ex - 1) + 127
    byte = np.clip(np.where(amax > 0, byte, 1), 1, 254)
    scaled = (w * np.exp2(127.0 - byte)[:, None, :]).reshape(k, n).astype(np.float32)
    by_word = np.ascontiguousarray(scaled.reshape(k // 512, 128, 4, n).transpose(0, 1, 3, 2))
    if fmt == "e4m3":
        words = by_word.astype(ml_dtypes.float8_e4m3fn).view(np.uint8)
    else:
        c = by_word.astype(ml_dtypes.float4_e2m1fn).view(np.uint8) & 0xF
        words = (c[..., 0::2] | (c[..., 1::2] << 4)).reshape(k // 512, 128, 2 * n)
    return np.ascontiguousarray(words), np.ascontiguousarray(byte.astype(np.uint8).reshape(k // 512, 16, n))


def unpack_weight(words, scales, fmt):
    g, _, n = scales.shape
    words = np.ascontiguousarray(words).reshape(g, 128, n, -1)
    if fmt == "e4m3":
        vals = words.view(ml_dtypes.float8_e4m3fn).astype(np.float64)
    else:
        nib = np.empty((g, 128, n, 4), np.uint8)
        nib[..., 0::2] = words & 0xF
        nib[..., 1::2] = words >> 4
        vals = E2M1[nib]
    vals = vals * np.repeat(np.exp2(scales.astype(np.float64) - 127.0), 8, axis=1)[..., None]
    return vals.transpose(0, 1, 3, 2).reshape(g * 512, n)


def gelu(v):
    return 0.5 * v * (1.0 + np.tanh(np.sqrt(2.0 / np.pi) * (v + 0.044715 * v**3)))


def striped8(idx):
    return np.concatenate([v.reshape(-1, 16).T for v in idx]).astype(np.uint16)


def unstriped8(offs):
    return np.stack([offs[16 * g:16 * g + 16].T.reshape(-1) for g in range(8)]).astype(np.int64)


def heads(h, wgt, idx8):
    r = np.arange(h.shape[0])
    return wgt[r // 4 % 128] * h[r[:, None], idx8[r % 512 // 64]]


def put_heads(h, wgs, idx8, t2):
    r = np.arange(h.shape[0])
    page = np.zeros((h.shape[0], t2))
    page[r[:, None], idx8[r % 512 // 64]] = wgs[r // 4 % 128] * h
    return page


K, T, S, H, P, N, T2 = 1024, 4096, 1024, 1024, 512, 512, 1024

def setup_inputs():
    n = np.random.standard_normal
    s = mx_kscale(K)[:, None]
    u = mx_kscale(H)[:, None]
    d = {}
    d["tab_words"], d["tab_scales"] = pack_weight(n((K, T)) * s, "e4m3")
    d["w1"] = (1.6 * n((K, H)) / K ** 0.5 / s).astype(np.float32)
    d["gain"] = (np.exp(0.3 * n(H)) * u[:, 0]).astype(np.float32)
    d["w2_words"], d["w2_scales"] = pack_weight(n((H, H)) / H ** 0.5 / u * u.T, "e2m1")
    d["zone"] = (0.8 * n(H) * u[:, 0]).astype(np.float32)
    d["w3"] = (n((H, N)) / H ** 0.5 / u).astype(np.float32)
    d["wgt"] = np.repeat(np.random.uniform(0.5, 2.0, (8, P)), 16, axis=0).astype(np.float32)
    d["wgo"] = np.repeat(np.random.uniform(0.5, 2.0, (8, P)), 16, axis=0).astype(np.float32)
    d["offs"] = striped(np.random.permutation(T)[:S])
    d["offs2"] = striped8(np.stack([np.random.permutation(S)[:P] for _ in range(8)]))
    d["offs3"] = striped8(np.stack([np.random.permutation(T2)[:P] for _ in range(8)]))
    return d

def reference(tab_words, tab_scales, w1, gain, w2_words, w2_scales, zone, w3, wgt, wgo, offs, offs2, offs3):
    v = unpack_weight(tab_words, tab_scales, "e4m3")[:, unstriped(offs)]
    w2 = unpack_weight(w2_words, w2_scales, "e2m1")
    b = mxq(f64(w1), 0, "e4m3").T @ v
    f = b / (1.0 + np.exp(-b)) * f64(gain)[:, None]
    h = f + (w2.T @ mxq(f, 0, "e4m3"))
    x = heads(h, f64(wgt), unstriped8(offs2)) + f64(zone)[:, None]
    e = mxq(f64(w3), 0, "e4m3").T @ mxq(x, 0, "e4m3")
    y = np.sqrt(1.0 + np.square(e))
    return put_heads(y, f64(wgo), unstriped8(offs3), T2)

@@ -1,0 +1,272 @@
+from contextlib import ExitStack
+
+import concourse.mybir as mybir
+
+K, T, S, H, M, N, T2 = 1024, 4096, 1024, 1024, 512, 512, 1024
+FLOPS = 2 * K * H * S + 2 * H * H * S + 2 * H * N * M
+
+F32 = mybir.dt.float32
+BF16 = mybir.dt.bfloat16
+I32 = mybir.dt.int32
+U32 = mybir.dt.uint32
+U16 = mybir.dt.uint16
+U8 = mybir.dt.uint8
+FP8X4 = mybir.dt.float8_e4m3fn_x4
+FP4X4 = mybir.dt.float4_e2m1fn_x4
+ACT = mybir.ActivationFunctionType
+ALU = mybir.AluOpType
+
+P = 128
+PACK = 4
+KP = P * PACK
+SH = S // 2
+MH = M // 2
+
+
+def tile_list_fibre_draw_scores_kernel(tc, tab_words, tab_scales, w1, gain, w2_words, w2_scales, zone, w3, wgt, wgo, offs, offs2, offs3, out):
+    nc = tc.nc
+    with ExitStack() as ctx:
+        sb = ctx.enter_context(tc.tile_pool(name="sb", bufs=1))
+        ps = ctx.enter_context(tc.psum_pool(name="ps", bufs=8))
+
+        shared = ctx.enter_context(tc.tile_pool(name="shared", bufs=1))
+
+        def new(name, shape, dtype, tag=None, bufs=1):
+            return sb.tile(shape, dtype, name=name, tag=tag or name, bufs=bufs, align_bytes=64)
+
+        idx = sb.tile([P, S // 16], U16, name="idx")
+        idx2 = sb.tile([P, M // 16], U16, name="idx2")
+        idx3 = sb.tile([P, M // 16], U16, name="idx3")
+
+        tab_sc = new("tab_sc", [P, T], U8)
+        w2_sc_raw = new("w2_sc_raw", [P, 2 * H], U8)
+        nc.vector.memset(tab_sc[:].bitcast(I32), 0)
+        nc.vector.memset(w2_sc_raw[:].bitcast(I32), 0)
+        pages = [new(f"page{t}", [P, T2], F32) for t in range(PACK)]
+        for t in range(PACK):
+            nc.vector.memset(pages[t][:], 0.0)
+
+        def load_weight(name, w, a, b):
+            raw = new(name, [P, PACK, KP], F32, "w_raw", 4)
+            nc.sync.dma_start(out=raw[:], in_=w[a * KP : (a + 1) * KP, b * KP : (b + 1) * KP].rearrange("(p j) c -> p j c", j=PACK))
+            return raw
+
+        def load_table(a, cuts):
+            words = shared.tile([P, T], I32, name=f"tab{a}", offset=a * T * 4)
+            src = tab_words[a].rearrange("p t i -> p (t i)").bitcast(I32)
+            for c0, c1 in zip(cuts[:-1], cuts[1:]):
+                nc.sync.dma_start(out=words[:, c0:c1], in_=src[:, c0:c1])
+            return words
+
+        nc.sync.dma_start(idx[:], offs)
+        gain_sb = new("gain_sb", [P, 2, PACK], F32)
+        nc.sync.dma_start(out=gain_sb[:], in_=gain.rearrange("(b p t) -> p b t", b=2, t=PACK))
+        zone_sb = new("zone_sb", [P, 2, PACK], F32)
+        nc.sync.dma_start(out=zone_sb[:], in_=zone.rearrange("(b p t) -> p b t", b=2, t=PACK))
+        nc.sync.dma_start(idx2[:], offs2)
+        nc.sync.dma_start(idx3[:], offs3)
+        tab, w1_raw = {}, {}
+        tab[0] = load_table(0, [0, 1024, 2048, 4096])
+        for q in range(4):
+            nc.sync.dma_start(out=tab_sc[32 * q : 32 * q + 8, :].bitcast(I32), in_=tab_scales[:, 4 * q : 4 * q + 4, :].bitcast(I32))
+        w1_raw[0, 0] = load_weight("w1_00", w1, 0, 0)
+        w2_raw = new("w2_raw", [P, 2, H // 2], I32)
+        nc.sync.dma_start(out=w2_raw[:], in_=w2_words.bitcast(I32).rearrange("a p c -> p a c"))
+        tab[1] = load_table(1, [0, 4096])
+        for q in range(4):
+            nc.sync.dma_start(
+                out=w2_sc_raw[32 * q : 32 * q + 4, :].bitcast(I32).rearrange("p (a c) -> p a c", a=2),
+                in_=w2_scales[:, 4 * q : 4 * q + 4, :].bitcast(I32).rearrange("a r c -> r a c"),
+            )
+        w1_raw[1, 0] = load_weight("w1_10", w1, 1, 0)
+        w1_raw[0, 1] = load_weight("w1_01", w1, 0, 1)
+        w1_raw[1, 1] = load_weight("w1_11", w1, 1, 1)
+        w3_raw = [load_weight(f"w3_{b}", w3, b, 0) for b in range(2)]
+        wgt_sb = new("wgt_sb", [P, M], F32)
+        nc.sync.dma_start(out=wgt_sb[:], in_=wgt)
+        wgo_sb = new("wgo_sb", [P, M], F32)
+        nc.sync.dma_start(out=wgo_sb[:], in_=wgo)
+
+        def quantize(name, grouped, width):
+            codes = new(name + "_codes", [P, width], U32)
+            scales = new(name + "_scales", [P, width], U8)
+            nc.vector.quantize_mx(out=codes[:].bitcast(FP8X4), scales=scales[:], in_=grouped[:])
+            return codes, scales
+
+        def round_weight(name, raw, u, on_scalar):
+            grouped = new(name + "_bf", [P, 2 * P * PACK], BF16, "w_bf", 4)
+            dst = grouped[:].rearrange("p (e q j) -> p q j e", e=2, j=PACK)
+            src = raw[:].rearrange("p j (q t) -> p q j t", t=PACK)[:, :, :, 2 * u : 2 * u + 2]
+            if on_scalar:
+                nc.scalar.copy(out=dst, in_=src)
+            else:
+                nc.vector.tensor_copy(out=dst, in_=src)
+            return grouped
+
+        def prepare_weight(name, raw, scalar_halves):
+            grouped = [round_weight(f"{name}_{u}", raw, u, u in scalar_halves) for u in range(2)]
+            return [quantize(f"{name}_{u}", grouped[u], 2 * P) for u in range(2)]
+
+        def stationary(halves, t):
+            codes, scales = halves[t // 2]
+            cols = slice((t % 2) * P, (t % 2 + 1) * P)
+            return codes[:, cols].bitcast(FP8X4), scales[:, cols]
+
+        v_words, v_scales = {}, {}
+
+        def gather_words(a):
+            for h in range(2):
+                v_words[a, h] = new(f"v{a}{h}", [P, SH], U32)
+                nc.vector.tensor_copy(v_words[a, h][:], tab[a][:].bitcast(U32).indirect(idx[:, 32 * h : 32 * (h + 1)]))
+
+        for h in range(2):
+            v_scales[h] = new(f"vs{h}", [P, SH], U8)
+            nc.vector.tensor_copy(v_scales[h][:], tab_sc[:].indirect(idx[:, 32 * h : 32 * (h + 1)]))
+        gather_words(0)
+        w1q = {}
+        w1q[0, 0] = prepare_weight("w1q00", w1_raw[0, 0], (0, 1))
+        gather_words(1)
+        w1q[1, 0] = prepare_weight("w1q10", w1_raw[1, 0], (1,))
+
+        w2_codes = [new(f"w2c{a}", [P, 2 * H], U8) for a in range(2)]
+        w2_sc = new("w2_sc", [P, 2 * H], U8)
+        nc.vector.tensor_copy(
+            out=w2_sc[:].rearrange("p (g t c i) -> p g c t i", g=4, t=PACK, i=16),
+            in_=w2_sc_raw[:].rearrange("p (g c i t) -> p g c t i", g=4, t=PACK, i=16),
+        )
+        for a in range(2):
+            nc.vector.tensor_copy(
+                out=w2_codes[a][:].bitcast(U16).rearrange("p (b t c i) -> p b c t i", b=2, t=PACK, i=8),
+                in_=w2_raw[:, a, :].bitcast(U16).rearrange("p (b c i t) -> p b c t i", b=2, t=PACK, i=8),
+            )
+
+        s = {}
+
+        def first_product(b, h):
+            s[b, h] = new(f"s{b}{h}", [P, PACK, SH], F32)
+            for t in range(PACK):
+                acc = ps.tile([P, SH], F32, name="acc")
+                for a in range(2):
+                    codes, scales = stationary(w1q[a, b], t)
+                    nc.tensor.matmul_mx(
+                        out=acc[:], lhsT=codes, lhsT_scale=scales,
+                        rhs=v_words[a, h][:].bitcast(FP8X4), rhs_scale=v_scales[h][4 * a : P, :],
+                        start=(a == 0), stop=(a == 1),
+                    )
+                nc.scalar.activation(out=s[b, h][:, t, :], in_=acc[:], func=ACT.Silu)
+
+        def by_four(ap_planes):
+            return ap_planes.rearrange("p t (c i) -> p c t i", i=4)
+
+        def woven(tile):
+            return tile[:].rearrange("p (c i t) -> p c t i", i=4, t=PACK)
+
+        fq = {}
+
+        def features_on_vector(b, h):
+            grouped = new(f"f{b}{h}_bf", [P, SH * PACK], BF16, "f_bf", 2)
+            factor = gain_sb[:, b, :].unsqueeze(1).unsqueeze(3).to_broadcast([P, SH // 4, PACK, 4])
+            nc.vector.tensor_tensor(woven(grouped), by_four(s[b, h][:]), factor, ALU.mult)
+            fq[b, h] = quantize(f"fq{b}{h}", grouped, SH)
+
+        def features_on_scalar(b, h):
+            planes = new(f"f{b}{h}_pl", [P, PACK, SH], BF16)
+            for t in range(PACK):
+                nc.scalar.activation(out=planes[:, t, :], in_=s[b, h][:, t, :], func=ACT.Copy, scale=gain_sb[:, b, t : t + 1])
+            grouped = new(f"f{b}{h}_bf", [P, SH * PACK], BF16, "f_bf", 2)
+            nc.scalar.copy(out=woven(grouped), in_=by_four(planes[:]))
+            fq[b, h] = quantize(f"fq{b}{h}", grouped, SH)
+
+        first_product(0, 0)
+        first_product(0, 1)
+        w1q[0, 1] = prepare_weight("w1q01", w1_raw[0, 1], ())
+        w1q[1, 1] = prepare_weight("w1q11", w1_raw[1, 1], ())
+        first_product(1, 0)
+        first_product(1, 1)
+        features_on_vector(0, 0)
+        features_on_vector(1, 0)
+        features_on_vector(0, 1)
+        features_on_scalar(1, 1)
+
+        hid = {(b, t): shared.tile([P, S], F32, name=f"h{b}{t}", offset=(b * PACK + t) * S * 4) for b in range(2) for t in range(PACK)}
+
+        def second_pass(acc, a, b, t, h):
+            col = b * KP + t * P
+            codes, scales = fq[a, h]
+            nc.tensor.matmul_mx(
+                out=acc[:], lhsT=w2_codes[a][:, 2 * col : 2 * (col + P)].bitcast(FP4X4),
+                lhsT_scale=w2_sc[:, a * H + col : a * H + col + P],
+                rhs=codes[:].bitcast(FP8X4), rhs_scale=scales[:],
+                start=(a == 0), stop=(a == 1),
+            )
+
+        def residual(acc, b, t, h):
+            nc.vector.scalar_tensor_tensor(
+                out=hid[b, t][:, h * SH : (h + 1) * SH], in0=s[b, h][:, t, :], scalar=gain_sb[:, b, t : t + 1],
+                in1=acc[:], op0=ALU.mult, op1=ALU.add,
+            )
+
+        picked, x_planes, xq = {}, {}, {}
+
+        def pick(b, t, m):
+            if t == 0:
+                picked[b, m] = new(f"g{b}{m}", [P, PACK, MH], F32, "picked", 2)
+                x_planes[b, m] = new(f"x{b}{m}_pl", [P, PACK, MH], BF16, "x_pl", 2)
+            nc.vector.tensor_tensor(
+                picked[b, m][:, t, :], hid[b, t][:].indirect(idx2[:, 16 * m : 16 * (m + 1)]),
+                wgt_sb[:, m * MH : (m + 1) * MH], ALU.mult,
+            )
+            nc.scalar.activation(out=x_planes[b, m][:, t, :], in_=picked[b, m][:, t, :], func=ACT.Identity, bias=zone_sb[:, b, t : t + 1])
+            if t == PACK - 1:
+                grouped = new(f"x{b}{m}_bf", [P, MH * PACK], BF16, "x_bf", 2)
+                nc.scalar.copy(out=woven(grouped), in_=by_four(x_planes[b, m][:]))
+                xq[b, m] = quantize(f"xq{b}{m}", grouped, MH)
+
+        rows = [(b, t) for b in range(2) for t in range(PACK)]
+        accs = {}
+        for b, t in rows:
+            accs[b, t] = ps.tile([P, SH], F32, name="acc")
+            second_pass(accs[b, t], 0, b, t, 0)
+        for b, t in rows:
+            second_pass(accs[b, t], 1, b, t, 0)
+            residual(accs[b, t], b, t, 0)
+        w3q = [prepare_weight(f"w3q{b}", w3_raw[b], (0, 1)) for b in range(2)]
+        for b, t in rows:
+            acc = ps.tile([P, SH], F32, name="acc")
+            for a in range(2):
+                second_pass(acc, a, b, t, 1)
+            residual(acc, b, t, 1)
+            pick(b, t, 0)
+
+        y = {}
+
+        def scores(m):
+            for t in range(PACK):
+                acc = ps.tile([P, MH], F32, name="acc")
+                for b in range(2):
+                    codes, scales = stationary(w3q[b], t)
+                    nc.tensor.matmul_mx(
+                        out=acc[:], lhsT=codes, lhsT_scale=scales,
+                        rhs=xq[b, m][0][:].bitcast(FP8X4), rhs_scale=xq[b, m][1][:],
+                        start=(b == 0), stop=(b == 1),
+                    )
+                square = new(f"sq{m}{t}", [P, MH], F32, "square", 2)
+                nc.scalar.activation(out=square[:], in_=acc[:], func=ACT.Square)
+                y[m, t] = new(f"y{m}{t}", [P, MH], F32)
+                nc.scalar.activation(out=y[m, t][:], in_=square[:], func=ACT.Sqrt, bias=1.0)
+
+        def place(m, t):
+            nc.vector.tensor_tensor(
+                pages[t][:].indirect(idx3[:, 16 * m : 16 * (m + 1)]), y[m, t][:], wgo_sb[:, m * MH : (m + 1) * MH], ALU.mult
+            )
+
+        scores(0)
+        for b, t in rows:
+            pick(b, t, 1)
+        scores(1)
+        for t in range(PACK):
+            place(0, t)
+        out_rows = out.rearrange("(p t) c -> p t c", t=PACK)
+        for t in range(PACK):
+            place(1, t)
+            nc.sync.dma_start(out=out_rows[:, t, :], in_=pages[t][:])

@@ -42,9 +42,8 @@ def tile_list_fibre_draw_scores_kernel(tc, tab_words, tab_scales, w1, gain, w2_w
         w2_sc_raw = new("w2_sc_raw", [P, 2 * H], U8)
         nc.vector.memset(tab_sc[:].bitcast(I32), 0)
         nc.vector.memset(w2_sc_raw[:].bitcast(I32), 0)
-        pages = [new(f"page{t}", [P, T2], F32) for t in range(PACK)]
-        for t in range(PACK):
-            nc.vector.memset(pages[t][:], 0.0)
+        for q in range(4):
+            nc.gpsimd.dma_start(out=tab_sc[32 * q : 32 * q + 8, :].bitcast(I32), in_=tab_scales[:, 4 * q : 4 * q + 4, :].bitcast(I32))
 
         def load_weight(name, w, a, b):
             raw = new(name, [P, PACK, KP], F32, "w_raw", 4)
@@ -59,31 +58,30 @@ def tile_list_fibre_draw_scores_kernel(tc, tab_words, tab_scales, w1, gain, w2_w
             return words
 
         nc.sync.dma_start(idx[:], offs)
-        gain_sb = new("gain_sb", [P, 2, PACK], F32)
-        nc.sync.dma_start(out=gain_sb[:], in_=gain.rearrange("(b p t) -> p b t", b=2, t=PACK))
-        zone_sb = new("zone_sb", [P, 2, PACK], F32)
-        nc.sync.dma_start(out=zone_sb[:], in_=zone.rearrange("(b p t) -> p b t", b=2, t=PACK))
-        nc.sync.dma_start(idx2[:], offs2)
-        nc.sync.dma_start(idx3[:], offs3)
+        w2_raw = [new(f"w2_raw{a}", [P, H // 2], I32) for a in range(2)]
+        for a in range(2):
+            nc.sync.dma_start(out=w2_raw[a][:], in_=w2_words[a].bitcast(I32))
         tab, w1_raw = {}, {}
-        tab[0] = load_table(0, [0, 1024, 2048, 4096])
-        for q in range(4):
-            nc.sync.dma_start(out=tab_sc[32 * q : 32 * q + 8, :].bitcast(I32), in_=tab_scales[:, 4 * q : 4 * q + 4, :].bitcast(I32))
+        tab[0] = load_table(0, [0, 768, 1536, 2304, 3072, 4096])
         w1_raw[0, 0] = load_weight("w1_00", w1, 0, 0)
-        w2_raw = new("w2_raw", [P, 2, H // 2], I32)
-        nc.sync.dma_start(out=w2_raw[:], in_=w2_words.bitcast(I32).rearrange("a p c -> p a c"))
-        tab[1] = load_table(1, [0, 4096])
         for q in range(4):
             nc.sync.dma_start(
                 out=w2_sc_raw[32 * q : 32 * q + 4, :].bitcast(I32).rearrange("p (a c) -> p a c", a=2),
                 in_=w2_scales[:, 4 * q : 4 * q + 4, :].bitcast(I32).rearrange("a r c -> r a c"),
             )
+        gain_sb = new("gain_sb", [P, 2, PACK], F32)
+        nc.sync.dma_start(out=gain_sb[:], in_=gain.rearrange("(b p t) -> p b t", b=2, t=PACK))
+        tab[1] = load_table(1, [0, 4096])
         w1_raw[1, 0] = load_weight("w1_10", w1, 1, 0)
         w1_raw[0, 1] = load_weight("w1_01", w1, 0, 1)
         w1_raw[1, 1] = load_weight("w1_11", w1, 1, 1)
         w3_raw = [load_weight(f"w3_{b}", w3, b, 0) for b in range(2)]
+        zone_sb = new("zone_sb", [P, 2, PACK], F32)
+        nc.sync.dma_start(out=zone_sb[:], in_=zone.rearrange("(b p t) -> p b t", b=2, t=PACK))
+        nc.sync.dma_start(idx2[:], offs2)
         wgt_sb = new("wgt_sb", [P, M], F32)
         nc.sync.dma_start(out=wgt_sb[:], in_=wgt)
+        nc.sync.dma_start(idx3[:], offs3)
         wgo_sb = new("wgo_sb", [P, M], F32)
         nc.sync.dma_start(out=wgo_sb[:], in_=wgo)
 
@@ -93,23 +91,29 @@ def tile_list_fibre_draw_scores_kernel(tc, tab_words, tab_scales, w1, gain, w2_w
             nc.vector.quantize_mx(out=codes[:].bitcast(FP8X4), scales=scales[:], in_=grouped[:])
             return codes, scales
 
-        def round_weight(name, raw, u, on_scalar):
-            grouped = new(name + "_bf", [P, 2 * P * PACK], BF16, "w_bf", 4)
-            dst = grouped[:].rearrange("p (e q j) -> p q j e", e=2, j=PACK)
-            src = raw[:].rearrange("p j (q t) -> p q j t", t=PACK)[:, :, :, 2 * u : 2 * u + 2]
-            if on_scalar:
-                nc.scalar.copy(out=dst, in_=src)
-            else:
-                nc.vector.tensor_copy(out=dst, in_=src)
-            return grouped
+        def prepare_weight(name, raw, scalar_halves, whole):
+            grouped = new(name + "_bf", [P, KP * PACK], BF16, "w_bf", 2)
+            codes = new(name + "_codes", [P, KP], U32)
+            scales = new(name + "_scales", [P, KP], U8)
+            half = KP * PACK // 2
+            for u in range(2):
+                dst = grouped[:, u * half : (u + 1) * half].rearrange("p (e q j) -> p q j e", e=2, j=PACK)
+                src = raw[:].rearrange("p j (q t) -> p q j t", t=PACK)[:, :, :, 2 * u : 2 * u + 2]
+                if u in scalar_halves:
+                    nc.scalar.copy(out=dst, in_=src)
+                else:
+                    nc.vector.tensor_copy(out=dst, in_=src)
+            width = KP if whole else KP // 2
+            for c in range(0, KP, width):
+                nc.vector.quantize_mx(
+                    out=codes[:, c : c + width].bitcast(FP8X4), scales=scales[:, c : c + width],
+                    in_=grouped[:, PACK * c : PACK * (c + width)],
+                )
+            return codes, scales
 
-        def prepare_weight(name, raw, scalar_halves):
-            grouped = [round_weight(f"{name}_{u}", raw, u, u in scalar_halves) for u in range(2)]
-            return [quantize(f"{name}_{u}", grouped[u], 2 * P) for u in range(2)]
-
-        def stationary(halves, t):
-            codes, scales = halves[t // 2]
-            cols = slice((t % 2) * P, (t % 2 + 1) * P)
+        def stationary(weight, t):
+            codes, scales = weight
+            cols = slice(t * P, (t + 1) * P)
             return codes[:, cols].bitcast(FP8X4), scales[:, cols]
 
         v_words, v_scales = {}, {}
@@ -119,26 +123,25 @@ def tile_list_fibre_draw_scores_kernel(tc, tab_words, tab_scales, w1, gain, w2_w
                 v_words[a, h] = new(f"v{a}{h}", [P, SH], U32)
                 nc.vector.tensor_copy(v_words[a, h][:], tab[a][:].bitcast(U32).indirect(idx[:, 32 * h : 32 * (h + 1)]))
 
+        w2_codes = [new(f"w2c{a}", [P, 2 * H], U8) for a in range(2)]
+        for a in range(2):
+            nc.vector.tensor_copy(
+                out=w2_codes[a][:].bitcast(U16).rearrange("p (b t c i) -> p b c t i", b=2, t=PACK, i=8),
+                in_=w2_raw[a][:].bitcast(U16).rearrange("p (b c i t) -> p b c t i", b=2, t=PACK, i=8),
+            )
         for h in range(2):
             v_scales[h] = new(f"vs{h}", [P, SH], U8)
             nc.vector.tensor_copy(v_scales[h][:], tab_sc[:].indirect(idx[:, 32 * h : 32 * (h + 1)]))
         gather_words(0)
         w1q = {}
-        w1q[0, 0] = prepare_weight("w1q00", w1_raw[0, 0], (0, 1))
-        gather_words(1)
-        w1q[1, 0] = prepare_weight("w1q10", w1_raw[1, 0], (1,))
-
-        w2_codes = [new(f"w2c{a}", [P, 2 * H], U8) for a in range(2)]
+        w1q[0, 0] = prepare_weight("w1q00", w1_raw[0, 0], (0, 1), True)
         w2_sc = new("w2_sc", [P, 2 * H], U8)
         nc.vector.tensor_copy(
             out=w2_sc[:].rearrange("p (g t c i) -> p g c t i", g=4, t=PACK, i=16),
             in_=w2_sc_raw[:].rearrange("p (g c i t) -> p g c t i", g=4, t=PACK, i=16),
         )
-        for a in range(2):
-            nc.vector.tensor_copy(
-                out=w2_codes[a][:].bitcast(U16).rearrange("p (b t c i) -> p b c t i", b=2, t=PACK, i=8),
-                in_=w2_raw[:, a, :].bitcast(U16).rearrange("p (b c i t) -> p b c t i", b=2, t=PACK, i=8),
-            )
+        gather_words(1)
+        w1q[1, 0] = prepare_weight("w1q10", w1_raw[1, 0], (1,), False)
 
         s = {}
 
@@ -155,38 +158,44 @@ def tile_list_fibre_draw_scores_kernel(tc, tab_words, tab_scales, w1, gain, w2_w
                     )
                 nc.scalar.activation(out=s[b, h][:, t, :], in_=acc[:], func=ACT.Silu)
 
-        def by_four(ap_planes):
-            return ap_planes.rearrange("p t (c i) -> p c t i", i=4)
+        def in_runs(planes, run):
+            return planes[:].rearrange("p t (c i) -> p c t i", i=run)
 
-        def woven(tile):
-            return tile[:].rearrange("p (c i t) -> p c t i", i=4, t=PACK)
+        def woven(tile, run):
+            return tile[:].rearrange("p (c i t) -> p c t i", i=run, t=PACK)
 
         fq = {}
 
         def features_on_vector(b, h):
-            grouped = new(f"f{b}{h}_bf", [P, SH * PACK], BF16, "f_bf", 2)
-            factor = gain_sb[:, b, :].unsqueeze(1).unsqueeze(3).to_broadcast([P, SH // 4, PACK, 4])
-            nc.vector.tensor_tensor(woven(grouped), by_four(s[b, h][:]), factor, ALU.mult)
+            grouped = new(f"f{b}{h}_bf", [P, SH * PACK], BF16, f"page{2 * h + b}")
+            factor = gain_sb[:, b, :].unsqueeze(1).unsqueeze(3).to_broadcast([P, SH // 2, PACK, 2])
+            nc.vector.tensor_tensor(woven(grouped, 2), in_runs(s[b, h], 2), factor, ALU.mult)
             fq[b, h] = quantize(f"fq{b}{h}", grouped, SH)
 
         def features_on_scalar(b, h):
             planes = new(f"f{b}{h}_pl", [P, PACK, SH], BF16)
             for t in range(PACK):
                 nc.scalar.activation(out=planes[:, t, :], in_=s[b, h][:, t, :], func=ACT.Copy, scale=gain_sb[:, b, t : t + 1])
-            grouped = new(f"f{b}{h}_bf", [P, SH * PACK], BF16, "f_bf", 2)
-            nc.scalar.copy(out=woven(grouped), in_=by_four(planes[:]))
+            grouped = new(f"f{b}{h}_bf", [P, SH * PACK], BF16, f"page{2 * h + b}")
+            nc.scalar.copy(out=woven(grouped, 4), in_=in_runs(planes, 4))
             fq[b, h] = quantize(f"fq{b}{h}", grouped, SH)
 
         first_product(0, 0)
+        w1q[0, 1] = prepare_weight("w1q01", w1_raw[0, 1], (), True)
+        w1q[1, 1] = prepare_weight("w1q11", w1_raw[1, 1], (1,), False)
         first_product(0, 1)
-        w1q[0, 1] = prepare_weight("w1q01", w1_raw[0, 1], ())
-        w1q[1, 1] = prepare_weight("w1q11", w1_raw[1, 1], ())
         first_product(1, 0)
         first_product(1, 1)
         features_on_vector(0, 0)
         features_on_vector(1, 0)
         features_on_vector(0, 1)
         features_on_scalar(1, 1)
+        one = new("one", [P, 1], F32)
+        nc.scalar.activation(out=one[:], in_=s[1, 1][:, PACK - 1, 0:1], func=ACT.Sqrt, scale=0.0, bias=1.0)
+
+        pages = [new(f"page{t}", [P, T2], F32) for t in range(PACK)]
+        for t in range(PACK):
+            nc.gpsimd.memset(pages[t][:], 0.0)
 
         hid = {(b, t): shared.tile([P, S], F32, name=f"h{b}{t}", offset=(b * PACK + t) * S * 4) for b in range(2) for t in range(PACK)}
 
@@ -206,20 +215,23 @@ def tile_list_fibre_draw_scores_kernel(tc, tab_words, tab_scales, w1, gain, w2_w
                 in1=acc[:], op0=ALU.mult, op1=ALU.add,
             )
 
-        picked, x_planes, xq = {}, {}, {}
+        x_planes, xq = {}, {}
 
         def pick(b, t, m):
+            if (b, t, m) == (0, 2, 1):
+                picked = new(f"g{b}{t}{m}", [P, MH], F32, "hold_a")
+            else:
+                picked = new(f"g{b}{t}{m}", [P, MH], F32, "picked", 8)
             if t == 0:
-                picked[b, m] = new(f"g{b}{m}", [P, PACK, MH], F32, "picked", 2)
                 x_planes[b, m] = new(f"x{b}{m}_pl", [P, PACK, MH], BF16, "x_pl", 2)
             nc.vector.tensor_tensor(
-                picked[b, m][:, t, :], hid[b, t][:].indirect(idx2[:, 16 * m : 16 * (m + 1)]),
+                picked[:], hid[b, t][:].indirect(idx2[:, 16 * m : 16 * (m + 1)]),
                 wgt_sb[:, m * MH : (m + 1) * MH], ALU.mult,
             )
-            nc.scalar.activation(out=x_planes[b, m][:, t, :], in_=picked[b, m][:, t, :], func=ACT.Identity, bias=zone_sb[:, b, t : t + 1])
+            nc.scalar.activation(out=x_planes[b, m][:, t, :], in_=picked[:], func=ACT.Identity, bias=zone_sb[:, b, t : t + 1])
             if t == PACK - 1:
-                grouped = new(f"x{b}{m}_bf", [P, MH * PACK], BF16, "x_bf", 2)
-                nc.scalar.copy(out=woven(grouped), in_=by_four(x_planes[b, m][:]))
+                grouped = new(f"x{b}{m}_bf", [P, MH * PACK], BF16, {(1, 0): "hold_a", (1, 1): "hold_b"}.get((b, m)))
+                nc.scalar.copy(out=woven(grouped, 4), in_=in_runs(x_planes[b, m], 4))
                 xq[b, m] = quantize(f"xq{b}{m}", grouped, MH)
 
         rows = [(b, t) for b in range(2) for t in range(PACK)]
@@ -230,15 +242,21 @@ def tile_list_fibre_draw_scores_kernel(tc, tab_words, tab_scales, w1, gain, w2_w
         for b, t in rows:
             second_pass(accs[b, t], 1, b, t, 0)
             residual(accs[b, t], b, t, 0)
-        w3q = [prepare_weight(f"w3q{b}", w3_raw[b], (0, 1)) for b in range(2)]
+        w3q = [prepare_weight(f"w3q{b}", w3_raw[b], (0, 1), True) for b in range(2)]
         for b, t in rows:
             acc = ps.tile([P, SH], F32, name="acc")
             for a in range(2):
                 second_pass(acc, a, b, t, 1)
             residual(acc, b, t, 1)
-            pick(b, t, 0)
+            if (b, t) != rows[0]:
+                pick(*rows[rows.index((b, t)) - 1], 0)
+        pick(*rows[-1], 0)
 
-        y = {}
+        y, square = {}, {}
+
+        def root(m, t):
+            y[m, t] = new(f"y{m}{t}", [P, MH], F32, "hold_b" if (m, t) == (0, 2) else None)
+            nc.scalar.activation(out=y[m, t][:], in_=square[m, t][:], func=ACT.Sqrt, bias=one[:])
 
         def scores(m):
             for t in range(PACK):
@@ -250,10 +268,10 @@ def tile_list_fibre_draw_scores_kernel(tc, tab_words, tab_scales, w1, gain, w2_w
                         rhs=xq[b, m][0][:].bitcast(FP8X4), rhs_scale=xq[b, m][1][:],
                         start=(b == 0), stop=(b == 1),
                     )
-                square = new(f"sq{m}{t}", [P, MH], F32, "square", 2)
-                nc.scalar.activation(out=square[:], in_=acc[:], func=ACT.Square)
-                y[m, t] = new(f"y{m}{t}", [P, MH], F32)
-                nc.scalar.activation(out=y[m, t][:], in_=square[:], func=ACT.Sqrt, bias=1.0)
+                square[m, t] = new(f"sq{m}{t}", [P, MH], F32, "square", 4)
+                nc.scalar.activation(out=square[m, t][:], in_=acc[:], func=ACT.Square)
+                if (m, t) != (0, 2):
+                    root(m, t)
 
         def place(m, t):
             nc.vector.tensor_tensor(
@@ -263,10 +281,11 @@ def tile_list_fibre_draw_scores_kernel(tc, tab_words, tab_scales, w1, gain, w2_w
         scores(0)
         for b, t in rows:
             pick(b, t, 1)
+        root(0, 2)
         scores(1)
-        for t in range(PACK):
+        for t in (0, 1, 3, 2):
             place(0, t)
         out_rows = out.rearrange("(p t) c -> p t c", t=PACK)
-        for t in range(PACK):
+        for t in (0, 1, 3, 2):
             place(1, t)
             nc.sync.dma_start(out=out_rows[:, t, :], in_=pages[t][:])

@@ -42,11 +42,15 @@ def tile_list_fibre_draw_scores_kernel(tc, tab_words, tab_scales, w1, gain, w2_w
         w2_sc_raw = new("w2_sc_raw", [P, 2 * H], U8)
         nc.vector.memset(tab_sc[:].bitcast(I32), 0)
         nc.vector.memset(w2_sc_raw[:].bitcast(I32), 0)
+        pages = [new(f"page{t}", [P, T2], F32) for t in range(PACK)]
+        for t in range(PACK):
+            nc.vector.memset(pages[t][:], 0.0)
+
         for q in range(4):
             nc.gpsimd.dma_start(out=tab_sc[32 * q : 32 * q + 8, :].bitcast(I32), in_=tab_scales[:, 4 * q : 4 * q + 4, :].bitcast(I32))
 
-        def load_weight(name, w, a, b):
-            raw = new(name, [P, PACK, KP], F32, "w_raw", 4)
+        def load_weight(name, w, a, b, tag="w_raw", bufs=3):
+            raw = new(name, [P, PACK, KP], F32, tag, bufs)
             nc.sync.dma_start(out=raw[:], in_=w[a * KP : (a + 1) * KP, b * KP : (b + 1) * KP].rearrange("(p j) c -> p j c", j=PACK))
             return raw
 
@@ -74,7 +78,7 @@ def tile_list_fibre_draw_scores_kernel(tc, tab_words, tab_scales, w1, gain, w2_w
         tab[1] = load_table(1, [0, 4096])
         w1_raw[1, 0] = load_weight("w1_10", w1, 1, 0)
         w1_raw[0, 1] = load_weight("w1_01", w1, 0, 1)
-        w1_raw[1, 1] = load_weight("w1_11", w1, 1, 1)
+        w1_raw[1, 1] = load_weight("w1_11", w1, 1, 1, "s01", 1)
         w3_raw = [load_weight(f"w3_{b}", w3, b, 0) for b in range(2)]
         zone_sb = new("zone_sb", [P, 2, PACK], F32)
         nc.sync.dma_start(out=zone_sb[:], in_=zone.rearrange("(b p t) -> p b t", b=2, t=PACK))
@@ -91,8 +95,9 @@ def tile_list_fibre_draw_scores_kernel(tc, tab_words, tab_scales, w1, gain, w2_w
             nc.vector.quantize_mx(out=codes[:].bitcast(FP8X4), scales=scales[:], in_=grouped[:])
             return codes, scales
 
-        def prepare_weight(name, raw, scalar_halves, whole):
-            grouped = new(name + "_bf", [P, KP * PACK], BF16, "w_bf", 2)
+        def prepare_weight(name, raw, scalar_halves, whole, grouped=None):
+            if grouped is None:
+                grouped = new(name + "_bf", [P, KP * PACK], BF16, "w_bf", 2)
             codes = new(name + "_codes", [P, KP], U32)
             scales = new(name + "_scales", [P, KP], U8)
             half = KP * PACK // 2
@@ -167,35 +172,33 @@ def tile_list_fibre_draw_scores_kernel(tc, tab_words, tab_scales, w1, gain, w2_w
         fq = {}
 
         def features_on_vector(b, h):
-            grouped = new(f"f{b}{h}_bf", [P, SH * PACK], BF16, f"page{2 * h + b}")
+            grouped = new(f"f{b}{h}_bf", [P, SH * PACK], BF16, f"f_bf{b}")
             factor = gain_sb[:, b, :].unsqueeze(1).unsqueeze(3).to_broadcast([P, SH // 2, PACK, 2])
             nc.vector.tensor_tensor(woven(grouped, 2), in_runs(s[b, h], 2), factor, ALU.mult)
             fq[b, h] = quantize(f"fq{b}{h}", grouped, SH)
 
         def features_on_scalar(b, h):
-            planes = new(f"f{b}{h}_pl", [P, PACK, SH], BF16)
+            planes = new(f"f{b}{h}_pl", [P, PACK, SH], BF16, "hold_w3")
             for t in range(PACK):
                 nc.scalar.activation(out=planes[:, t, :], in_=s[b, h][:, t, :], func=ACT.Copy, scale=gain_sb[:, b, t : t + 1])
-            grouped = new(f"f{b}{h}_bf", [P, SH * PACK], BF16, f"page{2 * h + b}")
+            grouped = new(f"f{b}{h}_bf", [P, SH * PACK], BF16, f"f_bf{b}")
             nc.scalar.copy(out=woven(grouped, 4), in_=in_runs(planes, 4))
             fq[b, h] = quantize(f"fq{b}{h}", grouped, SH)
+            return grouped
 
         first_product(0, 0)
         w1q[0, 1] = prepare_weight("w1q01", w1_raw[0, 1], (), True)
-        w1q[1, 1] = prepare_weight("w1q11", w1_raw[1, 1], (1,), False)
-        first_product(0, 1)
+        last_bf = new("w1q11_bf", [P, KP * PACK], BF16, "f_bf0")
+        w1q[1, 1] = prepare_weight("w1q11", w1_raw[1, 1], (1,), False, last_bf)
         first_product(1, 0)
+        first_product(0, 1)
         first_product(1, 1)
         features_on_vector(0, 0)
         features_on_vector(1, 0)
         features_on_vector(0, 1)
-        features_on_scalar(1, 1)
+        last_features = features_on_scalar(1, 1)
         one = new("one", [P, 1], F32)
-        nc.scalar.activation(out=one[:], in_=s[1, 1][:, PACK - 1, 0:1], func=ACT.Sqrt, scale=0.0, bias=1.0)
-
-        pages = [new(f"page{t}", [P, T2], F32) for t in range(PACK)]
-        for t in range(PACK):
-            nc.gpsimd.memset(pages[t][:], 0.0)
+        nc.scalar.activation(out=one[:], in_=last_features[:, 0:1], func=ACT.Sqrt, scale=0.0, bias=1.0)
 
         hid = {(b, t): shared.tile([P, S], F32, name=f"h{b}{t}", offset=(b * PACK + t) * S * 4) for b in range(2) for t in range(PACK)}
 
@@ -217,22 +220,33 @@ def tile_list_fibre_draw_scores_kernel(tc, tab_words, tab_scales, w1, gain, w2_w
 
         x_planes, xq = {}, {}
 
-        def pick(b, t, m):
-            if (b, t, m) == (0, 2, 1):
+        def pick(b, t, m, picked):
+            nc.vector.tensor_tensor(
+                picked, hid[b, t][:].indirect(idx2[:, 16 * m : 16 * (m + 1)]), wgt_sb[:, m * MH : (m + 1) * MH], ALU.mult
+            )
+
+        def pick_for_scalar(b, t, m):
+            if (b, t, m) == (0, 3, 1):
                 picked = new(f"g{b}{t}{m}", [P, MH], F32, "hold_a")
             else:
-                picked = new(f"g{b}{t}{m}", [P, MH], F32, "picked", 8)
+                picked = new(f"g{b}{t}{m}", [P, MH], F32, "picked", 6)
             if t == 0:
                 x_planes[b, m] = new(f"x{b}{m}_pl", [P, PACK, MH], BF16, "x_pl", 2)
-            nc.vector.tensor_tensor(
-                picked[:], hid[b, t][:].indirect(idx2[:, 16 * m : 16 * (m + 1)]),
-                wgt_sb[:, m * MH : (m + 1) * MH], ALU.mult,
-            )
+            pick(b, t, m, picked[:])
             nc.scalar.activation(out=x_planes[b, m][:, t, :], in_=picked[:], func=ACT.Identity, bias=zone_sb[:, b, t : t + 1])
             if t == PACK - 1:
-                grouped = new(f"x{b}{m}_bf", [P, MH * PACK], BF16, {(1, 0): "hold_a", (1, 1): "hold_b"}.get((b, m)))
+                grouped = new(f"x{b}{m}_bf", [P, MH * PACK], BF16, "hold_a" if (b, m) == (1, 0) else None)
                 nc.scalar.copy(out=woven(grouped, 4), in_=in_runs(x_planes[b, m], 4))
                 xq[b, m] = quantize(f"xq{b}{m}", grouped, MH)
+
+        def last_rows_on_vector(b, m):
+            picked = new("g_last", [P, PACK, MH], F32)
+            for t in range(PACK):
+                pick(b, t, m, picked[:, t, :])
+            grouped = new("x_last_bf", [P, MH * PACK], BF16)
+            offset = zone_sb[:, b, :].unsqueeze(1).unsqueeze(3).to_broadcast([P, MH // 2, PACK, 2])
+            nc.vector.tensor_tensor(woven(grouped, 2), in_runs(picked, 2), offset, ALU.add)
+            xq[b, m] = quantize(f"xq{b}{m}", grouped, MH)
 
         rows = [(b, t) for b in range(2) for t in range(PACK)]
         accs = {}
@@ -242,21 +256,18 @@ def tile_list_fibre_draw_scores_kernel(tc, tab_words, tab_scales, w1, gain, w2_w
         for b, t in rows:
             second_pass(accs[b, t], 1, b, t, 0)
             residual(accs[b, t], b, t, 0)
-        w3q = [prepare_weight(f"w3q{b}", w3_raw[b], (0, 1), True) for b in range(2)]
+        w3_bf = new("w3_bf", [P, 2 * KP * PACK], BF16, "hold_w3")
+        w3q = [prepare_weight(f"w3q{b}", w3_raw[b], (0, 1), True, w3_bf[:, b * KP * PACK : (b + 1) * KP * PACK]) for b in range(2)]
         for b, t in rows:
             acc = ps.tile([P, SH], F32, name="acc")
             for a in range(2):
                 second_pass(acc, a, b, t, 1)
             residual(acc, b, t, 1)
             if (b, t) != rows[0]:
-                pick(*rows[rows.index((b, t)) - 1], 0)
-        pick(*rows[-1], 0)
+                pick_for_scalar(*rows[rows.index((b, t)) - 1], 0)
+        pick_for_scalar(*rows[-1], 0)
 
-        y, square = {}, {}
-
-        def root(m, t):
-            y[m, t] = new(f"y{m}{t}", [P, MH], F32, "hold_b" if (m, t) == (0, 2) else None)
-            nc.scalar.activation(out=y[m, t][:], in_=square[m, t][:], func=ACT.Sqrt, bias=one[:])
+        y = {}
 
         def scores(m):
             for t in range(PACK):
@@ -268,24 +279,24 @@ def tile_list_fibre_draw_scores_kernel(tc, tab_words, tab_scales, w1, gain, w2_w
                         rhs=xq[b, m][0][:].bitcast(FP8X4), rhs_scale=xq[b, m][1][:],
                         start=(b == 0), stop=(b == 1),
                     )
-                square[m, t] = new(f"sq{m}{t}", [P, MH], F32, "square", 4)
-                nc.scalar.activation(out=square[m, t][:], in_=acc[:], func=ACT.Square)
-                if (m, t) != (0, 2):
-                    root(m, t)
+                square = new(f"sq{m}{t}", [P, MH], F32, "square", 2)
+                nc.scalar.activation(out=square[:], in_=acc[:], func=ACT.Square)
+                y[m, t] = new(f"y{m}{t}", [P, MH], F32)
+                nc.scalar.activation(out=y[m, t][:], in_=square[:], func=ACT.Sqrt, bias=one[:])
 
         def place(m, t):
             nc.vector.tensor_tensor(
                 pages[t][:].indirect(idx3[:, 16 * m : 16 * (m + 1)]), y[m, t][:], wgo_sb[:, m * MH : (m + 1) * MH], ALU.mult
             )
 
+        for t in range(PACK):
+            pick_for_scalar(0, t, 1)
+        last_rows_on_vector(1, 1)
         scores(0)
-        for b, t in rows:
-            pick(b, t, 1)
-        root(0, 2)
         scores(1)
-        for t in (0, 1, 3, 2):
+        for t in range(PACK):
             place(0, t)
         out_rows = out.rearrange("(p t) c -> p t c", t=PACK)
-        for t in (0, 1, 3, 2):
+        for t in range(PACK):
             place(1, t)
             nc.sync.dma_start(out=out_rows[:, t, :], in_=pages[t][:])

@@ -40,11 +40,8 @@ def tile_list_fibre_draw_scores_kernel(tc, tab_words, tab_scales, w1, gain, w2_w
 
         tab_sc = new("tab_sc", [P, T], U8)
         w2_sc_raw = new("w2_sc_raw", [P, 2 * H], U8)
-        nc.vector.memset(tab_sc[:].bitcast(I32), 0)
+        nc.gpsimd.memset(tab_sc[:].bitcast(I32), 0)
         nc.vector.memset(w2_sc_raw[:].bitcast(I32), 0)
-        pages = [new(f"page{t}", [P, T2], F32) for t in range(PACK)]
-        for t in range(PACK):
-            nc.vector.memset(pages[t][:], 0.0)
 
         for q in range(4):
             nc.gpsimd.dma_start(out=tab_sc[32 * q : 32 * q + 8, :].bitcast(I32), in_=tab_scales[:, 4 * q : 4 * q + 4, :].bitcast(I32))
@@ -134,10 +131,10 @@ def tile_list_fibre_draw_scores_kernel(tc, tab_words, tab_scales, w1, gain, w2_w
                 out=w2_codes[a][:].bitcast(U16).rearrange("p (b t c i) -> p b c t i", b=2, t=PACK, i=8),
                 in_=w2_raw[a][:].bitcast(U16).rearrange("p (b c i t) -> p b c t i", b=2, t=PACK, i=8),
             )
-        for h in range(2):
-            v_scales[h] = new(f"vs{h}", [P, SH], U8)
-            nc.vector.tensor_copy(v_scales[h][:], tab_sc[:].indirect(idx[:, 32 * h : 32 * (h + 1)]))
         gather_words(0)
+        for h in range(2):
+            v_scales[h] = shared.tile([P, SH], U8, name=f"vs{h}", offset=h * SH, align_bytes=64)
+            nc.vector.tensor_copy(v_scales[h][:], tab_sc[:].indirect(idx[:, 32 * h : 32 * (h + 1)]))
         w1q = {}
         w1q[0, 0] = prepare_weight("w1q00", w1_raw[0, 0], (0, 1), True)
         w2_sc = new("w2_sc", [P, 2 * H], U8)
@@ -172,7 +169,7 @@ def tile_list_fibre_draw_scores_kernel(tc, tab_words, tab_scales, w1, gain, w2_w
         fq = {}
 
         def features_on_vector(b, h):
-            grouped = new(f"f{b}{h}_bf", [P, SH * PACK], BF16, f"f_bf{b}")
+            grouped = new(f"f{b}{h}_bf", [P, SH * PACK], BF16, f"page{2 * h + b}")
             factor = gain_sb[:, b, :].unsqueeze(1).unsqueeze(3).to_broadcast([P, SH // 2, PACK, 2])
             nc.vector.tensor_tensor(woven(grouped, 2), in_runs(s[b, h], 2), factor, ALU.mult)
             fq[b, h] = quantize(f"fq{b}{h}", grouped, SH)
@@ -181,14 +178,14 @@ def tile_list_fibre_draw_scores_kernel(tc, tab_words, tab_scales, w1, gain, w2_w
             planes = new(f"f{b}{h}_pl", [P, PACK, SH], BF16, "hold_w3")
             for t in range(PACK):
                 nc.scalar.activation(out=planes[:, t, :], in_=s[b, h][:, t, :], func=ACT.Copy, scale=gain_sb[:, b, t : t + 1])
-            grouped = new(f"f{b}{h}_bf", [P, SH * PACK], BF16, f"f_bf{b}")
+            grouped = new(f"f{b}{h}_bf", [P, SH * PACK], BF16, f"page{2 * h + b}")
             nc.scalar.copy(out=woven(grouped, 4), in_=in_runs(planes, 4))
             fq[b, h] = quantize(f"fq{b}{h}", grouped, SH)
             return grouped
 
         first_product(0, 0)
         w1q[0, 1] = prepare_weight("w1q01", w1_raw[0, 1], (), True)
-        last_bf = new("w1q11_bf", [P, KP * PACK], BF16, "f_bf0")
+        last_bf = new("w1q11_bf", [P, KP * PACK], BF16, "page0")
         w1q[1, 1] = prepare_weight("w1q11", w1_raw[1, 1], (1,), False, last_bf)
         first_product(1, 0)
         first_product(0, 1)
@@ -199,6 +196,10 @@ def tile_list_fibre_draw_scores_kernel(tc, tab_words, tab_scales, w1, gain, w2_w
         last_features = features_on_scalar(1, 1)
         one = new("one", [P, 1], F32)
         nc.scalar.activation(out=one[:], in_=last_features[:, 0:1], func=ACT.Sqrt, scale=0.0, bias=1.0)
+
+        pages = [new(f"page{t}", [P, T2], F32) for t in range(PACK)]
+        for t in range(PACK):
+            nc.gpsimd.memset(pages[t][:], 0.0)
 
         hid = {(b, t): shared.tile([P, S], F32, name=f"h{b}{t}", offset=(b * PACK + t) * S * 4) for b in range(2) for t in range(PACK)}
 

from contextlib import ExitStack

import concourse.mybir as mybir

K, T, S, H, M, N, T2 = 1024, 4096, 1024, 1024, 512, 512, 1024
FLOPS = 2 * K * H * S + 2 * H * H * S + 2 * H * N * M

F32 = mybir.dt.float32
BF16 = mybir.dt.bfloat16
I32 = mybir.dt.int32
U32 = mybir.dt.uint32
U16 = mybir.dt.uint16
U8 = mybir.dt.uint8
FP8X4 = mybir.dt.float8_e4m3fn_x4
FP4X4 = mybir.dt.float4_e2m1fn_x4
ACT = mybir.ActivationFunctionType
ALU = mybir.AluOpType

P = 128
PACK = 4
KP = P * PACK
SH = S // 2
MH = M // 2


def tile_list_fibre_draw_scores_kernel(tc, tab_words, tab_scales, w1, gain, w2_words, w2_scales, zone, w3, wgt, wgo, offs, offs2, offs3, out):
    nc = tc.nc
    with ExitStack() as ctx:
        sb = ctx.enter_context(tc.tile_pool(name="sb", bufs=1))
        ps = ctx.enter_context(tc.psum_pool(name="ps", bufs=8))

        shared = ctx.enter_context(tc.tile_pool(name="shared", bufs=1))

        def new(name, shape, dtype, tag=None, bufs=1):
            return sb.tile(shape, dtype, name=name, tag=tag or name, bufs=bufs, align_bytes=64)

        idx = sb.tile([P, S // 16], U16, name="idx")
        idx2 = sb.tile([P, M // 16], U16, name="idx2")
        idx3 = sb.tile([P, M // 16], U16, name="idx3")

        tab_sc = new("tab_sc", [P, T], U8)
        w2_sc_raw = new("w2_sc_raw", [P, 2 * H], U8)
        nc.gpsimd.memset(tab_sc[:].bitcast(I32), 0)
        nc.vector.memset(w2_sc_raw[:].bitcast(I32), 0)

        for q in range(4):
            nc.gpsimd.dma_start(out=tab_sc[32 * q : 32 * q + 8, :].bitcast(I32), in_=tab_scales[:, 4 * q : 4 * q + 4, :].bitcast(I32))

        def load_weight(name, w, a, b, tag="w_raw", bufs=3):
            raw = new(name, [P, PACK, KP], F32, tag, bufs)
            nc.sync.dma_start(out=raw[:], in_=w[a * KP : (a + 1) * KP, b * KP : (b + 1) * KP].rearrange("(p j) c -> p j c", j=PACK))
            return raw

        def load_table(a, cuts):
            words = shared.tile([P, T], I32, name=f"tab{a}", offset=a * T * 4)
            src = tab_words[a].rearrange("p t i -> p (t i)").bitcast(I32)
            for c0, c1 in zip(cuts[:-1], cuts[1:]):
                nc.sync.dma_start(out=words[:, c0:c1], in_=src[:, c0:c1])
            return words

        nc.sync.dma_start(idx[:], offs)
        w2_raw = [new(f"w2_raw{a}", [P, H // 2], I32) for a in range(2)]
        for a in range(2):
            nc.sync.dma_start(out=w2_raw[a][:], in_=w2_words[a].bitcast(I32))
        tab, w1_raw = {}, {}
        tab[0] = load_table(0, [0, 768, 1536, 2304, 3072, 4096])
        w1_raw[0, 0] = load_weight("w1_00", w1, 0, 0)
        for q in range(4):
            nc.sync.dma_start(
                out=w2_sc_raw[32 * q : 32 * q + 4, :].bitcast(I32).rearrange("p (a c) -> p a c", a=2),
                in_=w2_scales[:, 4 * q : 4 * q + 4, :].bitcast(I32).rearrange("a r c -> r a c"),
            )
        gain_sb = new("gain_sb", [P, 2, PACK], F32)
        nc.sync.dma_start(out=gain_sb[:], in_=gain.rearrange("(b p t) -> p b t", b=2, t=PACK))
        tab[1] = load_table(1, [0, 4096])
        w1_raw[1, 0] = load_weight("w1_10", w1, 1, 0)
        w1_raw[0, 1] = load_weight("w1_01", w1, 0, 1)
        w1_raw[1, 1] = load_weight("w1_11", w1, 1, 1, "s01", 1)
        w3_raw = [load_weight(f"w3_{b}", w3, b, 0) for b in range(2)]
        zone_sb = new("zone_sb", [P, 2, PACK], F32)
        nc.sync.dma_start(out=zone_sb[:], in_=zone.rearrange("(b p t) -> p b t", b=2, t=PACK))
        nc.sync.dma_start(idx2[:], offs2)
        wgt_sb = new("wgt_sb", [P, M], F32)
        nc.sync.dma_start(out=wgt_sb[:], in_=wgt)
        nc.sync.dma_start(idx3[:], offs3)
        wgo_sb = new("wgo_sb", [P, M], F32)
        nc.sync.dma_start(out=wgo_sb[:], in_=wgo)

        def quantize(name, grouped, width):
            codes = new(name + "_codes", [P, width], U32)
            scales = new(name + "_scales", [P, width], U8)
            nc.vector.quantize_mx(out=codes[:].bitcast(FP8X4), scales=scales[:], in_=grouped[:])
            return codes, scales

        def prepare_weight(name, raw, scalar_halves, whole, grouped=None):
            if grouped is None:
                grouped = new(name + "_bf", [P, KP * PACK], BF16, "w_bf", 2)
            codes = new(name + "_codes", [P, KP], U32)
            scales = new(name + "_scales", [P, KP], U8)
            half = KP * PACK // 2
            for u in range(2):
                dst = grouped[:, u * half : (u + 1) * half].rearrange("p (e q j) -> p q j e", e=2, j=PACK)
                src = raw[:].rearrange("p j (q t) -> p q j t", t=PACK)[:, :, :, 2 * u : 2 * u + 2]
                if u in scalar_halves:
                    nc.scalar.copy(out=dst, in_=src)
                else:
                    nc.vector.tensor_copy(out=dst, in_=src)
            width = KP if whole else KP // 2
            for c in range(0, KP, width):
                nc.vector.quantize_mx(
                    out=codes[:, c : c + width].bitcast(FP8X4), scales=scales[:, c : c + width],
                    in_=grouped[:, PACK * c : PACK * (c + width)],
                )
            return codes, scales

        def stationary(weight, t):
            codes, scales = weight
            cols = slice(t * P, (t + 1) * P)
            return codes[:, cols].bitcast(FP8X4), scales[:, cols]

        v_words, v_scales = {}, {}

        def gather_words(a):
            for h in range(2):
                v_words[a, h] = new(f"v{a}{h}", [P, SH], U32)
                nc.vector.tensor_copy(v_words[a, h][:], tab[a][:].bitcast(U32).indirect(idx[:, 32 * h : 32 * (h + 1)]))

        w2_codes = [new(f"w2c{a}", [P, 2 * H], U8) for a in range(2)]
        for a in range(2):
            nc.vector.tensor_copy(
                out=w2_codes[a][:].bitcast(U16).rearrange("p (b t c i) -> p b c t i", b=2, t=PACK, i=8),
                in_=w2_raw[a][:].bitcast(U16).rearrange("p (b c i t) -> p b c t i", b=2, t=PACK, i=8),
            )
        gather_words(0)
        for h in range(2):
            v_scales[h] = shared.tile([P, SH], U8, name=f"vs{h}", offset=h * SH, align_bytes=64)
            nc.vector.tensor_copy(v_scales[h][:], tab_sc[:].indirect(idx[:, 32 * h : 32 * (h + 1)]))
        w1q = {}
        w1q[0, 0] = prepare_weight("w1q00", w1_raw[0, 0], (0, 1), True)
        w2_sc = new("w2_sc", [P, 2 * H], U8)
        nc.vector.tensor_copy(
            out=w2_sc[:].rearrange("p (g t c i) -> p g c t i", g=4, t=PACK, i=16),
            in_=w2_sc_raw[:].rearrange("p (g c i t) -> p g c t i", g=4, t=PACK, i=16),
        )
        gather_words(1)
        w1q[1, 0] = prepare_weight("w1q10", w1_raw[1, 0], (1,), False)

        s = {}

        def first_product(b, h):
            s[b, h] = new(f"s{b}{h}", [P, PACK, SH], F32)
            for t in range(PACK):
                acc = ps.tile([P, SH], F32, name="acc")
                for a in range(2):
                    codes, scales = stationary(w1q[a, b], t)
                    nc.tensor.matmul_mx(
                        out=acc[:], lhsT=codes, lhsT_scale=scales,
                        rhs=v_words[a, h][:].bitcast(FP8X4), rhs_scale=v_scales[h][4 * a : P, :],
                        start=(a == 0), stop=(a == 1),
                    )
                nc.scalar.activation(out=s[b, h][:, t, :], in_=acc[:], func=ACT.Silu)

        def in_runs(planes, run):
            return planes[:].rearrange("p t (c i) -> p c t i", i=run)

        def woven(tile, run):
            return tile[:].rearrange("p (c i t) -> p c t i", i=run, t=PACK)

        fq = {}

        def features_on_vector(b, h):
            grouped = new(f"f{b}{h}_bf", [P, SH * PACK], BF16, f"page{2 * h + b}")
            factor = gain_sb[:, b, :].unsqueeze(1).unsqueeze(3).to_broadcast([P, SH // 2, PACK, 2])
            nc.vector.tensor_tensor(woven(grouped, 2), in_runs(s[b, h], 2), factor, ALU.mult)
            fq[b, h] = quantize(f"fq{b}{h}", grouped, SH)

        def features_on_scalar(b, h):
            planes = new(f"f{b}{h}_pl", [P, PACK, SH], BF16, "hold_w3")
            for t in range(PACK):
                nc.scalar.activation(out=planes[:, t, :], in_=s[b, h][:, t, :], func=ACT.Copy, scale=gain_sb[:, b, t : t + 1])
            grouped = new(f"f{b}{h}_bf", [P, SH * PACK], BF16, f"page{2 * h + b}")
            nc.scalar.copy(out=woven(grouped, 4), in_=in_runs(planes, 4))
            fq[b, h] = quantize(f"fq{b}{h}", grouped, SH)
            return grouped

        first_product(0, 0)
        w1q[0, 1] = prepare_weight("w1q01", w1_raw[0, 1], (), True)
        last_bf = new("w1q11_bf", [P, KP * PACK], BF16, "page0")
        w1q[1, 1] = prepare_weight("w1q11", w1_raw[1, 1], (1,), False, last_bf)
        first_product(1, 0)
        first_product(0, 1)
        first_product(1, 1)
        features_on_vector(0, 0)
        features_on_vector(1, 0)
        features_on_vector(0, 1)
        last_features = features_on_scalar(1, 1)
        one = new("one", [P, 1], F32)
        nc.scalar.activation(out=one[:], in_=last_features[:, 0:1], func=ACT.Sqrt, scale=0.0, bias=1.0)

        pages = [new(f"page{t}", [P, T2], F32) for t in range(PACK)]
        for t in range(PACK):
            nc.gpsimd.memset(pages[t][:], 0.0)

        hid = {(b, t): shared.tile([P, S], F32, name=f"h{b}{t}", offset=(b * PACK + t) * S * 4) for b in range(2) for t in range(PACK)}

        def second_pass(acc, a, b, t, h):
            col = b * KP + t * P
            codes, scales = fq[a, h]
            nc.tensor.matmul_mx(
                out=acc[:], lhsT=w2_codes[a][:, 2 * col : 2 * (col + P)].bitcast(FP4X4),
                lhsT_scale=w2_sc[:, a * H + col : a * H + col + P],
                rhs=codes[:].bitcast(FP8X4), rhs_scale=scales[:],
                start=(a == 0), stop=(a == 1),
            )

        def residual(acc, b, t, h):
            nc.vector.scalar_tensor_tensor(
                out=hid[b, t][:, h * SH : (h + 1) * SH], in0=s[b, h][:, t, :], scalar=gain_sb[:, b, t : t + 1],
                in1=acc[:], op0=ALU.mult, op1=ALU.add,
            )

        x_planes, xq = {}, {}

        def pick(b, t, m, picked):
            nc.vector.tensor_tensor(
                picked, hid[b, t][:].indirect(idx2[:, 16 * m : 16 * (m + 1)]), wgt_sb[:, m * MH : (m + 1) * MH], ALU.mult
            )

        def pick_for_scalar(b, t, m):
            if (b, t, m) == (0, 3, 1):
                picked = new(f"g{b}{t}{m}", [P, MH], F32, "hold_a")
            else:
                picked = new(f"g{b}{t}{m}", [P, MH], F32, "picked", 6)
            if t == 0:
                x_planes[b, m] = new(f"x{b}{m}_pl", [P, PACK, MH], BF16, "x_pl", 2)
            pick(b, t, m, picked[:])
            nc.scalar.activation(out=x_planes[b, m][:, t, :], in_=picked[:], func=ACT.Identity, bias=zone_sb[:, b, t : t + 1])
            if t == PACK - 1:
                grouped = new(f"x{b}{m}_bf", [P, MH * PACK], BF16, "hold_a" if (b, m) == (1, 0) else None)
                nc.scalar.copy(out=woven(grouped, 4), in_=in_runs(x_planes[b, m], 4))
                xq[b, m] = quantize(f"xq{b}{m}", grouped, MH)

        def last_rows_on_vector(b, m):
            picked = new("g_last", [P, PACK, MH], F32)
            for t in range(PACK):
                pick(b, t, m, picked[:, t, :])
            grouped = new("x_last_bf", [P, MH * PACK], BF16)
            offset = zone_sb[:, b, :].unsqueeze(1).unsqueeze(3).to_broadcast([P, MH // 2, PACK, 2])
            nc.vector.tensor_tensor(woven(grouped, 2), in_runs(picked, 2), offset, ALU.add)
            xq[b, m] = quantize(f"xq{b}{m}", grouped, MH)

        rows = [(b, t) for b in range(2) for t in range(PACK)]
        accs = {}
        for b, t in rows:
            accs[b, t] = ps.tile([P, SH], F32, name="acc")
            second_pass(accs[b, t], 0, b, t, 0)
        for b, t in rows:
            second_pass(accs[b, t], 1, b, t, 0)
            residual(accs[b, t], b, t, 0)
        w3_bf = new("w3_bf", [P, 2 * KP * PACK], BF16, "hold_w3")
        w3q = [prepare_weight(f"w3q{b}", w3_raw[b], (0, 1), True, w3_bf[:, b * KP * PACK : (b + 1) * KP * PACK]) for b in range(2)]
        for b, t in rows:
            acc = ps.tile([P, SH], F32, name="acc")
            for a in range(2):
                second_pass(acc, a, b, t, 1)
            residual(acc, b, t, 1)
            if (b, t) != rows[0]:
                pick_for_scalar(*rows[rows.index((b, t)) - 1], 0)
        pick_for_scalar(*rows[-1], 0)

        y = {}

        def scores(m):
            for t in range(PACK):
                acc = ps.tile([P, MH], F32, name="acc")
                for b in range(2):
                    codes, scales = stationary(w3q[b], t)
                    nc.tensor.matmul_mx(
                        out=acc[:], lhsT=codes, lhsT_scale=scales,
                        rhs=xq[b, m][0][:].bitcast(FP8X4), rhs_scale=xq[b, m][1][:],
                        start=(b == 0), stop=(b == 1),
                    )
                square = new(f"sq{m}{t}", [P, MH], F32, "square", 2)
                nc.scalar.activation(out=square[:], in_=acc[:], func=ACT.Square)
                y[m, t] = new(f"y{m}{t}", [P, MH], F32)
                nc.scalar.activation(out=y[m, t][:], in_=square[:], func=ACT.Sqrt, bias=one[:])

        def place(m, t):
            nc.vector.tensor_tensor(
                pages[t][:].indirect(idx3[:, 16 * m : 16 * (m + 1)]), y[m, t][:], wgo_sb[:, m * MH : (m + 1) * MH], ALU.mult
            )

        for t in range(PACK):
            pick_for_scalar(0, t, 1)
        last_rows_on_vector(1, 1)
        scores(0)
        scores(1)
        for t in range(PACK):
            place(0, t)
        out_rows = out.rearrange("(p t) c -> p t c", t=PACK)
        for t in range(PACK):
            place(1, t)
            nc.sync.dma_start(out=out_rows[:, t, :], in_=pages[t][:])
